import numpy as np
import ml_dtypes


def mxq(x, axis, fmt="e4m3"):
    dtype, down = {"e4m3": (ml_dtypes.float8_e4m3fn, 7), "e5m2": (ml_dtypes.float8_e5m2, 14)}[fmt]
    v = np.moveaxis(np.asarray(x, np.float32).astype(ml_dtypes.bfloat16).astype(np.float64), axis, -1)
    blocks = v.reshape(v.shape[:-1] + (-1, 32))
    amax = np.abs(blocks).max(-1, keepdims=True)
    byte = np.maximum(np.where(amax > 0, np.frexp(amax)[1] - 1 + 127, 0) - down, 1)
    scale = np.exp2(byte - 127.0)
    codes = (blocks / scale).astype(np.float32).astype(dtype).astype(np.float64)
    return np.moveaxis((codes * scale).reshape(v.shape), -1, axis)


WIDE = False


def mx_kscale(k):
    if not WIDE:
        return np.ones(k)
    levels = np.array([10, -10, 5, -5, 0])
    if k % 512:
        return np.exp2(np.random.permutation(np.resize(levels, k // 32))).repeat(32)
    a = np.empty((k // 512, 16))
    for p in range(k // 512):
        a[p, :8] = np.random.permutation(np.resize(levels, 8))
        for g in range(8):
            far = levels[np.abs(levels - a[p, g]) >= 10]
            a[p, g + 8] = far[np.random.randint(len(far))]
    return np.exp2(a.ravel()).repeat(32)


def f64(x):
    return np.asarray(x).astype(np.float64)


def striped(idx):
    return np.tile(idx.reshape(-1, 16).T, (8, 1)).astype(np.uint16)


def unstriped(offs):
    return offs[:16].T.reshape(-1).astype(np.int64)


def striped8(idx):
    return np.concatenate([x.reshape(-1, 16).T for x in idx]).astype(np.uint16)


def runs(offs, k):
    lists = np.stack([offs[16 * r : 16 * r + 16].T.reshape(-1) for r in range(8)]).astype(np.int64)
    return lists[np.arange(k) % 512 // 64]


def pack_weight(w):
    k, n = w.shape
    w = f64(np.asarray(w, np.float32).astype(ml_dtypes.bfloat16)).reshape(k // 32, 32, n)
    amax = np.abs(w).max(1)
    byte = np.clip(np.where(amax > 0, np.frexp(amax)[1] - 1 + 127 - 7, 1), 1, 254)
    scaled = (w * np.exp2(127.0 - byte)[:, None, :]).reshape(k, n).astype(np.float32)
    words = np.ascontiguousarray(scaled.reshape(k // 512, 128, 4, n).transpose(0, 1, 3, 2)).astype(ml_dtypes.float8_e4m3fn).view(np.uint8)
    return words, np.ascontiguousarray(byte.astype(np.uint8).reshape(k // 512, 16, n))


def unpack_weight(words, scales):
    g, p, n, _ = words.shape
    vals = np.ascontiguousarray(words).view(ml_dtypes.float8_e4m3fn).astype(np.float64) * np.repeat(np.exp2(scales.astype(np.float64) - 127.0), 8, axis=1)[..., None]
    return vals.transpose(0, 1, 3, 2).reshape(g * 512, n)


E2M1 = np.array([0.0, 0.5, 1.0, 1.5, 2.0, 3.0, 4.0, 6.0, -0.0, -0.5, -1.0, -1.5, -2.0, -3.0, -4.0, -6.0])


def pack_fp4(w):
    k, n = w.shape
    w = f64(np.asarray(w, np.float32).astype(ml_dtypes.bfloat16)).reshape(k // 32, 32, n)
    amax = np.abs(w).max(1)
    mant, ex = np.frexp(amax / 6.0)
    byte = np.clip(np.where(amax > 0, np.where(mant > 0.5, ex, ex - 1) + 127, 1), 1, 254)
    scaled = (w * np.exp2(127.0 - byte)[:, None, :]).reshape(k, n).astype(np.float32)
    c = np.ascontiguousarray(scaled.reshape(k // 512, 128, 4, n).transpose(0, 1, 3, 2)).astype(ml_dtypes.float4_e2m1fn).view(np.uint8) & 0xF
    words = (c[..., 0::2] | (c[..., 1::2] << 4)).reshape(k // 512, 128, 2 * n)
    return np.ascontiguousarray(words), np.ascontiguousarray(byte.astype(np.uint8).reshape(k // 512, 16, n))


def unpack_fp4(words, scales):
    g, _, n = scales.shape
    words = np.ascontiguousarray(words).reshape(g, 128, n, 2)
    nib = np.empty((g, 128, n, 4), np.uint8)
    nib[..., 0::2] = words & 0xF
    nib[..., 1::2] = words >> 4
    vals = E2M1[nib] * np.repeat(np.exp2(scales.astype(np.float64) - 127.0), 8, axis=1)[..., None]
    return vals.transpose(0, 1, 3, 2).reshape(g * 512, n)


def sigmoid(v):
    return 1.0 / (1.0 + np.exp(-np.maximum(v, -700.0)))

def planes(y):
    n, m = y.shape
    v = y.astype(np.float32).astype(ml_dtypes.bfloat16).astype(np.float64).reshape(n // 32, 32, m)
    top = np.abs(v).max(1)
    byte = np.clip(np.where(top > 0, np.frexp(top)[1] - 1 + 127 - 7, 1), 1, 254)
    codes = (v * np.exp2(127.0 - byte)[:, None, :]).reshape(n, m).astype(np.float32).astype(ml_dtypes.float8_e4m3fn).view(np.uint8)
    words = codes.reshape(n // 512, 128, 4, m).transpose(0, 1, 3, 2)
    return np.ascontiguousarray(words), np.ascontiguousarray(byte.astype(np.uint8).reshape(n // 512, 16, m))


K, T, S, H, C = 512, 2048, 512, 512, 512


def setup_inputs():
    n = np.random.standard_normal
    s = mx_kscale(K)[:, None]
    packed_xT = pack_weight(n((K, T)) * s)
    packed_w1 = pack_fp4(n((K, H)) / np.sqrt(K) / s)
    return {
        "x_words": packed_xT[0],
        "x_scales": packed_xT[1],
        "w1_words": packed_w1[0],
        "w1_scales": packed_w1[1],
        "gs": (np.random.uniform(0.5, 1.5, (K, 1)) / s).astype(np.float32),
        "offs": striped(np.random.permutation(T)[:S]),
        "n1": striped8(np.stack([np.random.permutation(S) for _ in range(8)])),
        "n2": striped8(np.stack([np.random.permutation(S) for _ in range(8)])),
        "ca": striped(np.random.permutation(T)[:C]),
        "cb": striped(np.random.permutation(T)[:C]),
        "n3": striped8(np.stack([np.random.permutation(S) for _ in range(8)])),
        "n4": striped8(np.stack([np.random.permutation(S) for _ in range(8)])),
        "n5": striped8(np.stack([np.random.permutation(S) for _ in range(8)])),
    }


def reference(x_words, x_scales, w1_words, w1_scales, gs, offs, n1, n2, ca, cb, n3, n4, n5):
    x_cb = unpack_weight(x_words, x_scales)[:, unstriped(cb)]
    xq = unpack_weight(x_words, x_scales)[:, unstriped(offs)]
    y = unpack_fp4(w1_words, w1_scales).T @ xq
    z = f64(gs) * (y * (sigmoid(y[np.arange(H)[:, None], runs(n1, H)] - (y[np.arange(H)[:, None], runs(n2, H)]))))
    zq = mxq(z, 0, "e4m3")
    b = 0.0625 * (x_cb.T @ zq)
    x_ca = unpack_weight(x_words, x_scales)[:, unstriped(ca)]
    a = 0.0625 * (x_ca.T @ zq)
    out_0 = b * (a[np.arange(C)[:, None], runs(n3, C)] - a) + 0.5 * ((b[np.arange(C)[:, None], runs(n5, C)]) * (a[np.arange(C)[:, None], runs(n4, C)] - a))
    return (out_0,) + planes(out_0)

@@ -1,0 +1,236 @@
+from contextlib import ExitStack
+
+import concourse.mybir as mybir
+
+K, T, S = 512, 2048, 512
+FLOPS = 3 * 2 * 512 * 512 * 512
+
+F32 = mybir.dt.float32
+BF16 = mybir.dt.bfloat16
+I32 = mybir.dt.int32
+U32 = mybir.dt.uint32
+U16 = mybir.dt.uint16
+U8 = mybir.dt.uint8
+FP8X4 = mybir.dt.float8_e4m3fn_x4
+FP4X4 = mybir.dt.float4_e2m1fn_x4
+ALU = mybir.AluOpType
+ACT = mybir.ActivationFunctionType
+
+P = 128
+PACK = 4
+HALF = S // 2
+
+
+def tile_picked_ccmpflowbcmp_none_po_kernel(
+    tc, x_words, x_scales, w1_words, w1_scales, gs, offs, n1, n2, ca, cb, n3, n4, n5, out_0, out_1, out_2
+):
+    nc = tc.nc
+    with ExitStack() as ctx:
+        sb = ctx.enter_context(tc.tile_pool(name="sb", bufs=1))
+        ps = ctx.enter_context(tc.psum_pool(name="ps", bufs=1))
+
+        def tile(shape, dtype, name, tag=None):
+            return sb.tile(shape, dtype, name=name, tag=tag or name, align_bytes=64)
+
+        def load_list(src, name):
+            t = sb.tile([P, S // 16], U16, name=name)
+            nc.sync.dma_start(t[:], src)
+            return t
+
+        def load_scales(engine, dst, src):
+            for q in range(4):
+                engine.dma_start(dst[32 * q : 32 * q + 4, :].bitcast(I32), src[0, 4 * q : 4 * q + 4, :].bitcast(I32))
+
+        def deal_words(dst, src):
+            nc.vector.tensor_copy(
+                dst[:].rearrange("p (t c i) -> p c t i", t=PACK, i=4),
+                src[:].rearrange("p (c i t) -> p c t i", t=PACK, i=4),
+            )
+
+        def deal_scales(dst, src):
+            nc.vector.tensor_copy(
+                dst[:].rearrange("p (t c i) -> p c t i", t=PACK, i=16),
+                src[:].rearrange("p (c i t) -> p c t i", t=PACK, i=16),
+            )
+
+        xs = tile([P, T], U8, "xs")
+        w1s = tile([P, S], U8, "w1s")
+        zero = tile([P, 1], F32, "zero")
+        nc.vector.memset(xs[:].bitcast(I32), 0)
+        nc.vector.memset(w1s[:].bitcast(I32), 0)
+        nc.vector.memset(zero[:], 0.0)
+
+        l_offs = load_list(offs, "l_offs")
+        load_scales(nc.scalar, xs, x_scales)
+        w1w = tile([P, 2 * S], U8, "w1w")
+        nc.sync.dma_start(w1w[:].bitcast(I32), w1_words[0].bitcast(I32))
+        l_ca = load_list(ca, "l_ca")
+        l_n2 = load_list(n2, "l_n2")
+        xw = tile([P, T], U32, "xw")
+        nc.sync.dma_start(xw[:].bitcast(I32), x_words[0].rearrange("p n t -> p (n t)").bitcast(I32))
+        load_scales(nc.sync, w1s, w1_scales)
+        l_n1 = load_list(n1, "l_n1")
+        gain = tile([P, PACK], F32, "gain")
+        nc.sync.dma_start(gain[:], gs.rearrange("(p t) o -> p (t o)", t=PACK))
+        l_cb = load_list(cb, "l_cb")
+        l_n3 = load_list(n3, "l_n3")
+        l_n4 = load_list(n4, "l_n4")
+        l_n5 = load_list(n5, "l_n5")
+
+        win = [tile([P, 2 * S], F32, "win%d" % t) for t in range(PACK)]
+        for t in range(PACK):
+            nc.scalar.activation(win[t][:, S:], zero[:].to_broadcast([P, S]), ACT.Sigmoid)
+
+        w1w_d = tile([P, 2 * S], U8, "w1w_d")
+        nc.vector.tensor_copy(
+            w1w_d[:].rearrange("p (t c i b) -> p c t i b", t=PACK, i=8, b=2),
+            w1w[:].rearrange("p (c i t b) -> p c t i b", t=PACK, i=8, b=2),
+        )
+        xq_s = tile([P, S], U8, "xq_s")
+        nc.vector.tensor_copy(xq_s[:], xs[:].indirect(l_offs[:]))
+        xq_w = tile([P, S], U32, "xq_w")
+        nc.vector.tensor_copy(xq_w[:], xw[:].indirect(l_offs[:]))
+        w1s_d = tile([P, S], U8, "w1s_d")
+        deal_scales(w1s_d, w1s)
+        ca_s = tile([P, S], U8, "ca_s")
+        nc.vector.tensor_copy(ca_s[:], xs[:].indirect(l_ca[:]))
+        ca_w = tile([P, S], U32, "ca_w")
+        nc.vector.tensor_copy(ca_w[:], xw[:].indirect(l_ca[:]))
+
+        y_ps = [ps.tile([P, S], F32, name="y_ps%d" % t, tag="bank%d" % t) for t in range(PACK)]
+        for t in range(PACK):
+            nc.tensor.matmul_mx(
+                out=y_ps[t][:],
+                lhsT=w1w_d[:, 2 * P * t : 2 * P * (t + 1)].bitcast(FP4X4),
+                lhsT_scale=w1s_d[:, P * t : P * (t + 1)],
+                rhs=xq_w[:].bitcast(FP8X4),
+                rhs_scale=xq_s[:],
+                start=True,
+                stop=True,
+            )
+        for t in range(PACK):
+            nc.scalar.activation(win[t][:, :S], y_ps[t][:], ACT.Copy)
+        gy = tile([P, PACK * S], F32, "gy")
+        sig = tile([P, PACK * S], F32, "sig")
+        y2 = [tile([P, S], F32, "y2_%d" % t) for t in range(PACK)]
+        diff = [tile([P, S], F32, "diff%d" % t) for t in range(PACK)]
+        nc.vector.tensor_copy(y2[0][:], win[0][:].indirect(l_n2[:]))
+        for t in range(PACK):
+            if t + 1 < PACK:
+                nc.vector.tensor_copy(y2[t + 1][:], win[t + 1][:].indirect(l_n2[:]))
+            nc.vector.tensor_tensor(diff[t][:], win[t][:].indirect(l_n1[:]), y2[t][:], ALU.subtract)
+            nc.scalar.activation(gy[:, S * t : S * (t + 1)], y_ps[t][:], ACT.Copy, scale=gain[:, t : t + 1])
+            nc.scalar.activation(sig[:, S * t : S * (t + 1)], diff[t][:], ACT.Sigmoid)
+
+        cb_s = tile([P, S], U8, "cb_s", tag="y2_%d" % (PACK - 1))
+        nc.vector.tensor_copy(cb_s[:], xs[:].indirect(l_cb[:]))
+
+        z16 = tile([P, PACK * S], BF16, "z16")
+        nc.vector.tensor_tensor(
+            z16[:].rearrange("p (c i t) -> p c t i", t=PACK, i=2),
+            gy[:].rearrange("p (t c i) -> p c t i", t=PACK, i=2),
+            sig[:].rearrange("p (t c i) -> p c t i", t=PACK, i=2),
+            ALU.mult,
+        )
+        ca_wd = tile([P, S], U32, "ca_wd", tag="gy")
+        deal_words(ca_wd, ca_w)
+        ca_sd = tile([P, S], U8, "ca_sd", tag="sig")
+        deal_scales(ca_sd, ca_s)
+        zq_w = tile([P, S], U32, "zq_w")
+        zq_s = tile([P, S], U8, "zq_s")
+        nc.vector.quantize_mx(out=zq_w[:].bitcast(FP8X4), scales=zq_s[:], in_=z16[:])
+        cb_w = tile([P, S], U32, "cb_w", tag="z16")
+        nc.vector.tensor_copy(cb_w[:], xw[:].indirect(l_cb[:]))
+        cb_wd = tile([P, S], U32, "cb_wd")
+        deal_words(cb_wd, cb_w)
+        cb_sd = tile([P, S], U8, "cb_sd")
+        deal_scales(cb_sd, cb_s)
+
+        def score(dst, words, scales, t):
+            nc.tensor.matmul_mx(
+                out=dst[:],
+                lhsT=words[:, P * t : P * (t + 1)].bitcast(FP8X4),
+                lhsT_scale=scales[:, P * t : P * (t + 1)],
+                rhs=zq_w[:].bitcast(FP8X4),
+                rhs_scale=zq_s[:],
+                start=True,
+                stop=True,
+            )
+
+        a_ps = [ps.tile([P, S], F32, name="a_ps%d" % t, tag="bank%d" % t) for t in range(PACK)]
+        b_ps = [ps.tile([P, S], F32, name="b_ps%d" % t, tag="bank%d" % (PACK + t)) for t in range(PACK)]
+        for t in range(PACK):
+            score(a_ps[t], ca_wd, ca_sd, t)
+        for t in range(PACK):
+            score(b_ps[t], cb_wd, cb_sd, t)
+
+        hb = [tile([P, 2 * S], F32, "hb%d" % t) for t in range(PACK)]
+        for t in range(PACK):
+            nc.scalar.activation(win[t][:, :S], a_ps[t][:], ACT.Copy, scale=0.0625)
+            nc.scalar.activation(hb[t][:, S:], a_ps[t][:], ACT.Copy, scale=0.0625)
+            nc.scalar.activation(hb[t][:, :S], b_ps[t][:], ACT.Copy, scale=0.03125)
+
+        res = tile([P, PACK * S], F32, "res")
+        out_rows = out_0.rearrange("(p t) j -> p t j", t=PACK)
+        o16 = [tile([P, PACK * HALF], BF16, "o16_%d" % h) for h in range(2)]
+        oq_w = tile([P, S], U32, "oq_w")
+        oq_s = tile([P, S], U8, "oq_s")
+        out_w = out_1[0].rearrange("p n t -> p (n t)").bitcast(I32)
+
+        steps = [(t, 0, S) for t in range(PACK - 1)] + [(PACK - 1, 0, HALF), (PACK - 1, HALF, S)]
+        terms = {}
+
+        def lookups(n, t, lo, hi):
+            w = hi - lo
+            cols = slice(lo // 16, hi // 16)
+            d3 = tile([P, w], F32, "d3_%d" % n)
+            d4 = tile([P, w], F32, "d4_%d" % n)
+            a_here = hb[t][:, S + lo : S + hi]
+            nc.vector.tensor_tensor(d3[:], win[t][:].indirect(l_n3[:, cols]), a_here, ALU.subtract)
+            nc.vector.tensor_tensor(d4[:], win[t][:].indirect(l_n4[:, cols]), a_here, ALU.subtract)
+            terms[n] = (d3, d4)
+
+        def products(n, t, lo, hi):
+            w = hi - lo
+            cols = slice(lo // 16, hi // 16)
+            d3, d4 = terms[n]
+            m3 = tile([P, w], F32, "m3_%d" % n)
+            m5 = tile([P, w], F32, "m5_%d" % n)
+            nc.vector.scalar_tensor_tensor(m3[:], hb[t][:, lo:hi], 2.0, d3[:], ALU.mult, ALU.mult)
+            nc.vector.tensor_tensor(m5[:], hb[t][:].indirect(l_n5[:, cols]), d4[:], ALU.mult)
+            terms[n] = (m3, m5)
+
+        def total(n, t, lo, hi):
+            m3, m5 = terms[n]
+            dst = res[:, S * t + lo : S * t + hi]
+            nc.vector.tensor_tensor(dst, m3[:], m5[:], ALU.add)
+            nc.sync.dma_start(out_rows[:, t, lo:hi], dst)
+
+        def cast_views(h):
+            src = res[:].rearrange("p (t j) -> p t j", t=PACK)[:, :, HALF * h : HALF * (h + 1)]
+            return (
+                o16[h][:].rearrange("p (c i t) -> p c t i", t=PACK, i=2),
+                src.rearrange("p t (c i) -> p c t i", i=2),
+            )
+
+        def quantise(h):
+            cols = slice(HALF * h, HALF * (h + 1))
+            nc.vector.quantize_mx(out=oq_w[:, cols].bitcast(FP8X4), scales=oq_s[:, cols], in_=o16[h][:])
+            nc.sync.dma_start(out_w[:, cols], oq_w[:, cols].bitcast(I32))
+
+        for n, step in enumerate(steps):
+            lookups(n, *step)
+            if n > 0:
+                total(n - 1, *steps[n - 1])
+            if n == len(steps) - 1:
+                dst, src = cast_views(0)
+                nc.scalar.activation(dst, src, ACT.Copy)
+            products(n, *step)
+        total(len(steps) - 1, *steps[-1])
+        quantise(0)
+        dst, src = cast_views(1)
+        nc.vector.tensor_copy(dst, src)
+        quantise(1)
+        for q in range(4):
+            engine = nc.scalar if q % 2 == 0 else nc.sync
+            engine.dma_start(out_2[0, 4 * q : 4 * q + 4, :].bitcast(I32), oq_s[32 * q : 32 * q + 4, :].bitcast(I32))

@@ -1,6 +1,7 @@
 from contextlib import ExitStack
 
 import concourse.mybir as mybir
+from concourse.masks import make_identity
 
 K, T, S = 512, 2048, 512
 FLOPS = 3 * 2 * 512 * 512 * 512
@@ -37,8 +38,8 @@ def tile_picked_ccmpflowbcmp_none_po_kernel(
             nc.sync.dma_start(t[:], src)
             return t
 
-        def load_scales(engine, dst, src):
-            for q in range(4):
+        def load_scales(engines, dst, src):
+            for q, engine in enumerate(engines):
                 engine.dma_start(dst[32 * q : 32 * q + 4, :].bitcast(I32), src[0, 4 * q : 4 * q + 4, :].bitcast(I32))
 
         def deal_words(dst, src):
@@ -61,14 +62,14 @@ def tile_picked_ccmpflowbcmp_none_po_kernel(
         nc.vector.memset(zero[:], 0.0)
 
         l_offs = load_list(offs, "l_offs")
-        load_scales(nc.scalar, xs, x_scales)
+        load_scales([nc.sync] * 4, xs, x_scales)
         w1w = tile([P, 2 * S], U8, "w1w")
         nc.sync.dma_start(w1w[:].bitcast(I32), w1_words[0].bitcast(I32))
         l_ca = load_list(ca, "l_ca")
-        l_n2 = load_list(n2, "l_n2")
         xw = tile([P, T], U32, "xw")
         nc.sync.dma_start(xw[:].bitcast(I32), x_words[0].rearrange("p n t -> p (n t)").bitcast(I32))
-        load_scales(nc.sync, w1s, w1_scales)
+        load_scales([nc.sync] * 4, w1s, w1_scales)
+        l_n2 = load_list(n2, "l_n2")
         l_n1 = load_list(n1, "l_n1")
         gain = tile([P, PACK], F32, "gain")
         nc.sync.dma_start(gain[:], gs.rearrange("(p t) o -> p (t o)", t=PACK))
@@ -77,6 +78,8 @@ def tile_picked_ccmpflowbcmp_none_po_kernel(
         l_n4 = load_list(n4, "l_n4")
         l_n5 = load_list(n5, "l_n5")
 
+        ident = tile([P, P], F32, "ident")
+        make_identity(nc, ident[:])
         win = [tile([P, 2 * S], F32, "win%d" % t) for t in range(PACK)]
         for t in range(PACK):
             nc.scalar.activation(win[t][:, S:], zero[:].to_broadcast([P, S]), ACT.Sigmoid)
@@ -94,8 +97,8 @@ def tile_picked_ccmpflowbcmp_none_po_kernel(
         deal_scales(w1s_d, w1s)
         ca_s = tile([P, S], U8, "ca_s")
         nc.vector.tensor_copy(ca_s[:], xs[:].indirect(l_ca[:]))
-        ca_w = tile([P, S], U32, "ca_w")
-        nc.vector.tensor_copy(ca_w[:], xw[:].indirect(l_ca[:]))
+        ca_wd = tile([P, S], U32, "ca_wd", tag="w1s")
+        nc.vector.tensor_copy(ca_wd[:].rearrange("p (t m) -> p m t", t=PACK), xw[:].indirect(l_ca[:]))
 
         y_ps = [ps.tile([P, S], F32, name="y_ps%d" % t, tag="bank%d" % t) for t in range(PACK)]
         for t in range(PACK):
@@ -120,29 +123,30 @@ def tile_picked_ccmpflowbcmp_none_po_kernel(
                 nc.vector.tensor_copy(y2[t + 1][:], win[t + 1][:].indirect(l_n2[:]))
             nc.vector.tensor_tensor(diff[t][:], win[t][:].indirect(l_n1[:]), y2[t][:], ALU.subtract)
             nc.scalar.activation(gy[:, S * t : S * (t + 1)], y_ps[t][:], ACT.Copy, scale=gain[:, t : t + 1])
-            nc.scalar.activation(sig[:, S * t : S * (t + 1)], diff[t][:], ACT.Sigmoid)
+            for lo, hi in [(0, S)] if t + 1 < PACK else [(0, HALF), (HALF, S)]:
+                nc.scalar.activation(sig[:, S * t + lo : S * t + hi], diff[t][:, lo:hi], ACT.Sigmoid)
 
-        cb_s = tile([P, S], U8, "cb_s", tag="y2_%d" % (PACK - 1))
-        nc.vector.tensor_copy(cb_s[:], xs[:].indirect(l_cb[:]))
-
-        z16 = tile([P, PACK * S], BF16, "z16")
-        nc.vector.tensor_tensor(
-            z16[:].rearrange("p (c i t) -> p c t i", t=PACK, i=2),
-            gy[:].rearrange("p (t c i) -> p c t i", t=PACK, i=2),
-            sig[:].rearrange("p (t c i) -> p c t i", t=PACK, i=2),
-            ALU.mult,
-        )
-        ca_wd = tile([P, S], U32, "ca_wd", tag="gy")
-        deal_words(ca_wd, ca_w)
-        ca_sd = tile([P, S], U8, "ca_sd", tag="sig")
+        ca_sd = tile([P, S], U8, "ca_sd", tag="y2_%d" % (PACK - 1))
         deal_scales(ca_sd, ca_s)
+
+        def half_view(planes, h):
+            cols = planes[:].rearrange("p (t j) -> p t j", t=PACK)[:, :, HALF * h : HALF * (h + 1)]
+            return cols.rearrange("p t (c i) -> p c t i", i=2)
+
+        z16 = [tile([P, PACK * HALF], BF16, "z16_%d" % h) for h in range(2)]
+        for h in range(2):
+            nc.vector.tensor_tensor(
+                z16[h][:].rearrange("p (c i t) -> p c t i", t=PACK, i=2), half_view(gy, h), half_view(sig, h), ALU.mult
+            )
         zq_w = tile([P, S], U32, "zq_w")
         zq_s = tile([P, S], U8, "zq_s")
-        nc.vector.quantize_mx(out=zq_w[:].bitcast(FP8X4), scales=zq_s[:], in_=z16[:])
-        cb_w = tile([P, S], U32, "cb_w", tag="z16")
-        nc.vector.tensor_copy(cb_w[:], xw[:].indirect(l_cb[:]))
-        cb_wd = tile([P, S], U32, "cb_wd")
-        deal_words(cb_wd, cb_w)
+        for h in range(2):
+            cols = slice(HALF * h, HALF * (h + 1))
+            nc.vector.quantize_mx(out=zq_w[:, cols].bitcast(FP8X4), scales=zq_s[:, cols], in_=z16[h][:])
+        cb_s = tile([P, S], U8, "cb_s", tag="z16_0")
+        nc.vector.tensor_copy(cb_s[:], xs[:].indirect(l_cb[:]))
+        cb_wd = tile([P, S], U32, "cb_wd", tag="z16_1")
+        nc.vector.tensor_copy(cb_wd[:].rearrange("p (t m) -> p m t", t=PACK), xw[:].indirect(l_cb[:]))
         cb_sd = tile([P, S], U8, "cb_sd")
         deal_scales(cb_sd, cb_s)
 
@@ -203,7 +207,22 @@ def tile_picked_ccmpflowbcmp_none_po_kernel(
         def total(n, t, lo, hi):
             m3, m5 = terms[n]
             dst = res[:, S * t + lo : S * t + hi]
-            nc.vector.tensor_tensor(dst, m3[:], m5[:], ALU.add)
+            if t < PACK - 1:
+                turned_ps = ps.tile([P, S], F32, name="turned_ps%d" % t, tag="bank%d" % t)
+                for c in range(0, S, P):
+                    for term in (m3, m5):
+                        nc.tensor.matmul(
+                            turned_ps[:, c : c + P], term[:, c : c + P], ident[:],
+                            start=term is m3, stop=term is m5, is_transpose=True,
+                        )
+                turned = tile([P, S], F32, "turned%d" % t)
+                nc.scalar.activation(turned[:], turned_ps[:], ACT.Copy)
+                back_ps = ps.tile([P, S], F32, name="back_ps%d" % t, tag="bank%d" % (PACK + t))
+                for c in range(0, S, P):
+                    nc.tensor.transpose(back_ps[:, c : c + P], turned[:, c : c + P], ident[:])
+                nc.scalar.activation(dst, back_ps[:], ACT.Copy)
+            else:
+                nc.vector.tensor_tensor(dst, m3[:], m5[:], ALU.add)
             nc.sync.dma_start(out_rows[:, t, lo:hi], dst)
 
         def cast_views(h):

@@ -61,19 +61,19 @@ def tile_picked_ccmpflowbcmp_none_po_kernel(
         nc.vector.memset(w1s[:].bitcast(I32), 0)
         nc.vector.memset(zero[:], 0.0)
 
-        l_offs = load_list(offs, "l_offs")
-        load_scales([nc.sync] * 4, xs, x_scales)
         w1w = tile([P, 2 * S], U8, "w1w")
         nc.sync.dma_start(w1w[:].bitcast(I32), w1_words[0].bitcast(I32))
+        l_offs = load_list(offs, "l_offs")
+        load_scales([nc.scalar, nc.sync] * 2, xs, x_scales)
         l_ca = load_list(ca, "l_ca")
         xw = tile([P, T], U32, "xw")
         nc.sync.dma_start(xw[:].bitcast(I32), x_words[0].rearrange("p n t -> p (n t)").bitcast(I32))
         load_scales([nc.sync] * 4, w1s, w1_scales)
+        l_cb = load_list(cb, "l_cb")
         l_n2 = load_list(n2, "l_n2")
         l_n1 = load_list(n1, "l_n1")
         gain = tile([P, PACK], F32, "gain")
         nc.sync.dma_start(gain[:], gs.rearrange("(p t) o -> p (t o)", t=PACK))
-        l_cb = load_list(cb, "l_cb")
         l_n3 = load_list(n3, "l_n3")
         l_n4 = load_list(n4, "l_n4")
         l_n5 = load_list(n5, "l_n5")
@@ -100,6 +100,9 @@ def tile_picked_ccmpflowbcmp_none_po_kernel(
         ca_wd = tile([P, S], U32, "ca_wd", tag="w1s")
         nc.vector.tensor_copy(ca_wd[:].rearrange("p (t m) -> p m t", t=PACK), xw[:].indirect(l_ca[:]))
 
+        cb_s = tile([P, S], U8, "cb_s")
+        nc.vector.tensor_copy(cb_s[:], xs[:].indirect(l_cb[:]))
+
         y_ps = [ps.tile([P, S], F32, name="y_ps%d" % t, tag="bank%d" % t) for t in range(PACK)]
         for t in range(PACK):
             nc.tensor.matmul_mx(
@@ -121,7 +124,10 @@ def tile_picked_ccmpflowbcmp_none_po_kernel(
         for t in range(PACK):
             if t + 1 < PACK:
                 nc.vector.tensor_copy(y2[t + 1][:], win[t + 1][:].indirect(l_n2[:]))
-            nc.vector.tensor_tensor(diff[t][:], win[t][:].indirect(l_n1[:]), y2[t][:], ALU.subtract)
+            for lo, hi in [(0, S)] if t + 1 < PACK else [(0, HALF), (HALF, S)]:
+                nc.vector.tensor_tensor(
+                    diff[t][:, lo:hi], win[t][:].indirect(l_n1[:, lo // 16 : hi // 16]), y2[t][:, lo:hi], ALU.subtract
+                )
             nc.scalar.activation(gy[:, S * t : S * (t + 1)], y_ps[t][:], ACT.Copy, scale=gain[:, t : t + 1])
             for lo, hi in [(0, S)] if t + 1 < PACK else [(0, HALF), (HALF, S)]:
                 nc.scalar.activation(sig[:, S * t + lo : S * t + hi], diff[t][:, lo:hi], ACT.Sigmoid)
@@ -143,35 +149,37 @@ def tile_picked_ccmpflowbcmp_none_po_kernel(
         for h in range(2):
             cols = slice(HALF * h, HALF * (h + 1))
             nc.vector.quantize_mx(out=zq_w[:, cols].bitcast(FP8X4), scales=zq_s[:, cols], in_=z16[h][:])
-        cb_s = tile([P, S], U8, "cb_s", tag="z16_0")
-        nc.vector.tensor_copy(cb_s[:], xs[:].indirect(l_cb[:]))
         cb_wd = tile([P, S], U32, "cb_wd", tag="z16_1")
         nc.vector.tensor_copy(cb_wd[:].rearrange("p (t m) -> p m t", t=PACK), xw[:].indirect(l_cb[:]))
-        cb_sd = tile([P, S], U8, "cb_sd")
+        cb_sd = tile([P, S], U8, "cb_sd", tag="z16_0")
         deal_scales(cb_sd, cb_s)
 
-        def score(dst, words, scales, t):
+        def score(bank, words, scales, t, lo, hi):
+            acc = ps.tile([P, hi - lo], F32, name="acc", tag="bank%d" % bank)
             nc.tensor.matmul_mx(
-                out=dst[:],
+                out=acc[:],
                 lhsT=words[:, P * t : P * (t + 1)].bitcast(FP8X4),
                 lhsT_scale=scales[:, P * t : P * (t + 1)],
-                rhs=zq_w[:].bitcast(FP8X4),
-                rhs_scale=zq_s[:],
+                rhs=zq_w[:, lo:hi].bitcast(FP8X4),
+                rhs_scale=zq_s[:, lo:hi],
                 start=True,
                 stop=True,
             )
+            return acc
 
-        a_ps = [ps.tile([P, S], F32, name="a_ps%d" % t, tag="bank%d" % t) for t in range(PACK)]
-        b_ps = [ps.tile([P, S], F32, name="b_ps%d" % t, tag="bank%d" % (PACK + t)) for t in range(PACK)]
-        for t in range(PACK):
-            score(a_ps[t], ca_wd, ca_sd, t)
-        for t in range(PACK):
-            score(b_ps[t], cb_wd, cb_sd, t)
-
+        a_parts = [(PACK, 0, 0, HALF), (0, 0, HALF, S)] + [(t, t, 0, S) for t in range(1, PACK)]
+        a_ps = [score(bank, ca_wd, ca_sd, t, lo, hi) for bank, t, lo, hi in a_parts]
         hb = [tile([P, 2 * S], F32, "hb%d" % t) for t in range(PACK)]
+
+        def leave_a(n):
+            bank, t, lo, hi = a_parts[n]
+            nc.scalar.activation(win[t][:, lo:hi], a_ps[n][:], ACT.Copy, scale=0.0625)
+            nc.scalar.activation(hb[t][:, S + lo : S + hi], a_ps[n][:], ACT.Copy, scale=0.0625)
+
+        leave_a(0)
+        b_ps = [score(PACK + t, cb_wd, cb_sd, t, 0, S) for t in range(PACK)]
         for t in range(PACK):
-            nc.scalar.activation(win[t][:, :S], a_ps[t][:], ACT.Copy, scale=0.0625)
-            nc.scalar.activation(hb[t][:, S:], a_ps[t][:], ACT.Copy, scale=0.0625)
+            leave_a(t + 1)
             nc.scalar.activation(hb[t][:, :S], b_ps[t][:], ACT.Copy, scale=0.03125)
 
         res = tile([P, PACK * S], F32, "res")
@@ -190,7 +198,13 @@ def tile_picked_ccmpflowbcmp_none_po_kernel(
             d3 = tile([P, w], F32, "d3_%d" % n)
             d4 = tile([P, w], F32, "d4_%d" % n)
             a_here = hb[t][:, S + lo : S + hi]
-            nc.vector.tensor_tensor(d3[:], win[t][:].indirect(l_n3[:, cols]), a_here, ALU.subtract)
+            for c0, c1 in [(0, HALF), (HALF, S)] if n == 0 else [(lo, hi)]:
+                nc.vector.tensor_tensor(
+                    d3[:, c0 - lo : c1 - lo],
+                    win[t][:].indirect(l_n3[:, c0 // 16 : c1 // 16]),
+                    hb[t][:, S + c0 : S + c1],
+                    ALU.subtract,
+                )
             nc.vector.tensor_tensor(d4[:], win[t][:].indirect(l_n4[:, cols]), a_here, ALU.subtract)
             terms[n] = (d3, d4)
 
@@ -245,10 +259,11 @@ def tile_picked_ccmpflowbcmp_none_po_kernel(
                 dst, src = cast_views(0)
                 nc.scalar.activation(dst, src, ACT.Copy)
             products(n, *step)
-        total(len(steps) - 1, *steps[-1])
-        quantise(0)
         dst, src = cast_views(1)
-        nc.vector.tensor_copy(dst, src)
+        nc.scalar.activation(dst[:, :, 0:2, :], src[:, :, 0:2, :], ACT.Copy)
+        quantise(0)
+        total(len(steps) - 1, *steps[-1])
+        nc.vector.tensor_copy(dst[:, :, 2:4, :], src[:, :, 2:4, :])
         quantise(1)
         for q in range(4):
             engine = nc.scalar if q % 2 == 0 else nc.sync

@@ -48,8 +48,8 @@ def tile_picked_ccmpflowbcmp_none_po_kernel(
                 src[:].rearrange("p (c i t) -> p c t i", t=PACK, i=4),
             )
 
-        def deal_scales(dst, src):
-            nc.vector.tensor_copy(
+        def deal_scales(dst, src, engine=nc.vector):
+            engine.tensor_copy(
                 dst[:].rearrange("p (t c i) -> p c t i", t=PACK, i=16),
                 src[:].rearrange("p (c i t) -> p c t i", t=PACK, i=16),
             )
@@ -61,9 +61,9 @@ def tile_picked_ccmpflowbcmp_none_po_kernel(
         nc.vector.memset(w1s[:].bitcast(I32), 0)
         nc.vector.memset(zero[:], 0.0)
 
+        l_offs = load_list(offs, "l_offs")
         w1w = tile([P, 2 * S], U8, "w1w")
         nc.sync.dma_start(w1w[:].bitcast(I32), w1_words[0].bitcast(I32))
-        l_offs = load_list(offs, "l_offs")
         load_scales([nc.scalar, nc.sync] * 2, xs, x_scales)
         l_ca = load_list(ca, "l_ca")
         xw = tile([P, T], U32, "xw")
@@ -85,7 +85,7 @@ def tile_picked_ccmpflowbcmp_none_po_kernel(
             nc.scalar.activation(win[t][:, S:], zero[:].to_broadcast([P, S]), ACT.Sigmoid)
 
         w1w_d = tile([P, 2 * S], U8, "w1w_d")
-        nc.vector.tensor_copy(
+        nc.gpsimd.tensor_copy(
             w1w_d[:].rearrange("p (t c i b) -> p c t i b", t=PACK, i=8, b=2),
             w1w[:].rearrange("p (c i t b) -> p c t i b", t=PACK, i=8, b=2),
         )
@@ -94,10 +94,10 @@ def tile_picked_ccmpflowbcmp_none_po_kernel(
         xq_w = tile([P, S], U32, "xq_w")
         nc.vector.tensor_copy(xq_w[:], xw[:].indirect(l_offs[:]))
         w1s_d = tile([P, S], U8, "w1s_d")
-        deal_scales(w1s_d, w1s)
+        deal_scales(w1s_d, w1s, nc.gpsimd)
         ca_s = tile([P, S], U8, "ca_s")
         nc.vector.tensor_copy(ca_s[:], xs[:].indirect(l_ca[:]))
-        ca_wd = tile([P, S], U32, "ca_wd", tag="w1s")
+        ca_wd = tile([P, S], U32, "ca_wd")
         nc.vector.tensor_copy(ca_wd[:].rearrange("p (t m) -> p m t", t=PACK), xw[:].indirect(l_ca[:]))
 
         cb_s = tile([P, S], U8, "cb_s")
@@ -252,17 +252,17 @@ def tile_picked_ccmpflowbcmp_none_po_kernel(
             nc.sync.dma_start(out_w[:, cols], oq_w[:, cols].bitcast(I32))
 
         for n, step in enumerate(steps):
-            lookups(n, *step)
             if n > 0:
                 total(n - 1, *steps[n - 1])
+            lookups(n, *step)
             if n == len(steps) - 1:
                 dst, src = cast_views(0)
                 nc.scalar.activation(dst, src, ACT.Copy)
             products(n, *step)
         dst, src = cast_views(1)
         nc.scalar.activation(dst[:, :, 0:2, :], src[:, :, 0:2, :], ACT.Copy)
-        quantise(0)
         total(len(steps) - 1, *steps[-1])
+        quantise(0)
         nc.vector.tensor_copy(dst[:, :, 2:4, :], src[:, :, 2:4, :])
         quantise(1)
         for q in range(4):

from contextlib import ExitStack

import concourse.mybir as mybir
from concourse.masks import make_identity

K, T, S = 512, 2048, 512
FLOPS = 3 * 2 * 512 * 512 * 512

F32 = mybir.dt.float32
BF16 = mybir.dt.bfloat16
I32 = mybir.dt.int32
U32 = mybir.dt.uint32
U16 = mybir.dt.uint16
U8 = mybir.dt.uint8
FP8X4 = mybir.dt.float8_e4m3fn_x4
FP4X4 = mybir.dt.float4_e2m1fn_x4
ALU = mybir.AluOpType
ACT = mybir.ActivationFunctionType

P = 128
PACK = 4
HALF = S // 2


def tile_picked_ccmpflowbcmp_none_po_kernel(
    tc, x_words, x_scales, w1_words, w1_scales, gs, offs, n1, n2, ca, cb, n3, n4, n5, out_0, out_1, out_2
):
    nc = tc.nc
    with ExitStack() as ctx:
        sb = ctx.enter_context(tc.tile_pool(name="sb", bufs=1))
        ps = ctx.enter_context(tc.psum_pool(name="ps", bufs=1))

        def tile(shape, dtype, name, tag=None):
            return sb.tile(shape, dtype, name=name, tag=tag or name, align_bytes=64)

        def load_list(src, name):
            t = sb.tile([P, S // 16], U16, name=name)
            nc.sync.dma_start(t[:], src)
            return t

        def load_scales(engines, dst, src):
            for q, engine in enumerate(engines):
                engine.dma_start(dst[32 * q : 32 * q + 4, :].bitcast(I32), src[0, 4 * q : 4 * q + 4, :].bitcast(I32))

        def deal_words(dst, src):
            nc.vector.tensor_copy(
                dst[:].rearrange("p (t c i) -> p c t i", t=PACK, i=4),
                src[:].rearrange("p (c i t) -> p c t i", t=PACK, i=4),
            )

        def deal_scales(dst, src, engine=nc.vector):
            engine.tensor_copy(
                dst[:].rearrange("p (t c i) -> p c t i", t=PACK, i=16),
                src[:].rearrange("p (c i t) -> p c t i", t=PACK, i=16),
            )

        xs = tile([P, T], U8, "xs")
        w1s = tile([P, S], U8, "w1s")
        zero = tile([P, 1], F32, "zero")
        nc.vector.memset(xs[:].bitcast(I32), 0)
        nc.vector.memset(w1s[:].bitcast(I32), 0)
        nc.vector.memset(zero[:], 0.0)

        l_offs = load_list(offs, "l_offs")
        w1w = tile([P, 2 * S], U8, "w1w")
        nc.sync.dma_start(w1w[:].bitcast(I32), w1_words[0].bitcast(I32))
        load_scales([nc.scalar, nc.sync] * 2, xs, x_scales)
        l_ca = load_list(ca, "l_ca")
        xw = tile([P, T], U32, "xw")
        nc.sync.dma_start(xw[:].bitcast(I32), x_words[0].rearrange("p n t -> p (n t)").bitcast(I32))
        load_scales([nc.sync] * 4, w1s, w1_scales)
        l_cb = load_list(cb, "l_cb")
        l_n2 = load_list(n2, "l_n2")
        l_n1 = load_list(n1, "l_n1")
        gain = tile([P, PACK], F32, "gain")
        nc.sync.dma_start(gain[:], gs.rearrange("(p t) o -> p (t o)", t=PACK))
        l_n3 = load_list(n3, "l_n3")
        l_n4 = load_list(n4, "l_n4")
        l_n5 = load_list(n5, "l_n5")

        ident = tile([P, P], F32, "ident")
        make_identity(nc, ident[:])
        win = [tile([P, 2 * S], F32, "win%d" % t) for t in range(PACK)]
        for t in range(PACK):
            nc.scalar.activation(win[t][:, S:], zero[:].to_broadcast([P, S]), ACT.Sigmoid)

        w1w_d = tile([P, 2 * S], U8, "w1w_d")
        nc.gpsimd.tensor_copy(
            w1w_d[:].rearrange("p (t c i b) -> p c t i b", t=PACK, i=8, b=2),
            w1w[:].rearrange("p (c i t b) -> p c t i b", t=PACK, i=8, b=2),
        )
        xq_s = tile([P, S], U8, "xq_s")
        nc.vector.tensor_copy(xq_s[:], xs[:].indirect(l_offs[:]))
        xq_w = tile([P, S], U32, "xq_w")
        nc.vector.tensor_copy(xq_w[:], xw[:].indirect(l_offs[:]))
        w1s_d = tile([P, S], U8, "w1s_d")
        deal_scales(w1s_d, w1s, nc.gpsimd)
        ca_s = tile([P, S], U8, "ca_s")
        nc.vector.tensor_copy(ca_s[:], xs[:].indirect(l_ca[:]))
        ca_wd = tile([P, S], U32, "ca_wd")
        nc.vector.tensor_copy(ca_wd[:].rearrange("p (t m) -> p m t", t=PACK), xw[:].indirect(l_ca[:]))

        cb_s = tile([P, S], U8, "cb_s")
        nc.vector.tensor_copy(cb_s[:], xs[:].indirect(l_cb[:]))

        y_ps = [ps.tile([P, S], F32, name="y_ps%d" % t, tag="bank%d" % t) for t in range(PACK)]
        for t in range(PACK):
            nc.tensor.matmul_mx(
                out=y_ps[t][:],
                lhsT=w1w_d[:, 2 * P * t : 2 * P * (t + 1)].bitcast(FP4X4),
                lhsT_scale=w1s_d[:, P * t : P * (t + 1)],
                rhs=xq_w[:].bitcast(FP8X4),
                rhs_scale=xq_s[:],
                start=True,
                stop=True,
            )
        for t in range(PACK):
            nc.scalar.activation(win[t][:, :S], y_ps[t][:], ACT.Copy)
        gy = tile([P, PACK * S], F32, "gy")
        sig = tile([P, PACK * S], F32, "sig")
        y2 = [tile([P, S], F32, "y2_%d" % t) for t in range(PACK)]
        diff = [tile([P, S], F32, "diff%d" % t) for t in range(PACK)]
        nc.vector.tensor_copy(y2[0][:], win[0][:].indirect(l_n2[:]))
        for t in range(PACK):
            if t + 1 < PACK:
                nc.vector.tensor_copy(y2[t + 1][:], win[t + 1][:].indirect(l_n2[:]))
            for lo, hi in [(0, S)] if t + 1 < PACK else [(0, HALF), (HALF, S)]:
                nc.vector.tensor_tensor(
                    diff[t][:, lo:hi], win[t][:].indirect(l_n1[:, lo // 16 : hi // 16]), y2[t][:, lo:hi], ALU.subtract
                )
            nc.scalar.activation(gy[:, S * t : S * (t + 1)], y_ps[t][:], ACT.Copy, scale=gain[:, t : t + 1])
            for lo, hi in [(0, S)] if t + 1 < PACK else [(0, HALF), (HALF, S)]:
                nc.scalar.activation(sig[:, S * t + lo : S * t + hi], diff[t][:, lo:hi], ACT.Sigmoid)

        ca_sd = tile([P, S], U8, "ca_sd", tag="y2_%d" % (PACK - 1))
        deal_scales(ca_sd, ca_s)

        def half_view(planes, h):
            cols = planes[:].rearrange("p (t j) -> p t j", t=PACK)[:, :, HALF * h : HALF * (h + 1)]
            return cols.rearrange("p t (c i) -> p c t i", i=2)

        z16 = [tile([P, PACK * HALF], BF16, "z16_%d" % h) for h in range(2)]
        for h in range(2):
            nc.vector.tensor_tensor(
                z16[h][:].rearrange("p (c i t) -> p c t i", t=PACK, i=2), half_view(gy, h), half_view(sig, h), ALU.mult
            )
        zq_w = tile([P, S], U32, "zq_w")
        zq_s = tile([P, S], U8, "zq_s")
        for h in range(2):
            cols = slice(HALF * h, HALF * (h + 1))
            nc.vector.quantize_mx(out=zq_w[:, cols].bitcast(FP8X4), scales=zq_s[:, cols], in_=z16[h][:])
        cb_wd = tile([P, S], U32, "cb_wd", tag="z16_1")
        nc.vector.tensor_copy(cb_wd[:].rearrange("p (t m) -> p m t", t=PACK), xw[:].indirect(l_cb[:]))
        cb_sd = tile([P, S], U8, "cb_sd", tag="z16_0")
        deal_scales(cb_sd, cb_s)

        def score(bank, words, scales, t, lo, hi):
            acc = ps.tile([P, hi - lo], F32, name="acc", tag="bank%d" % bank)
            nc.tensor.matmul_mx(
                out=acc[:],
                lhsT=words[:, P * t : P * (t + 1)].bitcast(FP8X4),
                lhsT_scale=scales[:, P * t : P * (t + 1)],
                rhs=zq_w[:, lo:hi].bitcast(FP8X4),
                rhs_scale=zq_s[:, lo:hi],
                start=True,
                stop=True,
            )
            return acc

        a_parts = [(PACK, 0, 0, HALF), (0, 0, HALF, S)] + [(t, t, 0, S) for t in range(1, PACK)]
        a_ps = [score(bank, ca_wd, ca_sd, t, lo, hi) for bank, t, lo, hi in a_parts]
        hb = [tile([P, 2 * S], F32, "hb%d" % t) for t in range(PACK)]

        def leave_a(n):
            bank, t, lo, hi = a_parts[n]
            nc.scalar.activation(win[t][:, lo:hi], a_ps[n][:], ACT.Copy, scale=0.0625)
            nc.scalar.activation(hb[t][:, S + lo : S + hi], a_ps[n][:], ACT.Copy, scale=0.0625)

        leave_a(0)
        b_ps = [score(PACK + t, cb_wd, cb_sd, t, 0, S) for t in range(PACK)]
        for t in range(PACK):
            leave_a(t + 1)
            nc.scalar.activation(hb[t][:, :S], b_ps[t][:], ACT.Copy, scale=0.03125)

        res = tile([P, PACK * S], F32, "res")
        out_rows = out_0.rearrange("(p t) j -> p t j", t=PACK)
        o16 = [tile([P, PACK * HALF], BF16, "o16_%d" % h) for h in range(2)]
        oq_w = tile([P, S], U32, "oq_w")
        oq_s = tile([P, S], U8, "oq_s")
        out_w = out_1[0].rearrange("p n t -> p (n t)").bitcast(I32)

        steps = [(t, 0, S) for t in range(PACK - 1)] + [(PACK - 1, 0, HALF), (PACK - 1, HALF, S)]
        terms = {}

        def lookups(n, t, lo, hi):
            w = hi - lo
            cols = slice(lo // 16, hi // 16)
            d3 = tile([P, w], F32, "d3_%d" % n)
            d4 = tile([P, w], F32, "d4_%d" % n)
            a_here = hb[t][:, S + lo : S + hi]
            for c0, c1 in [(0, HALF), (HALF, S)] if n == 0 else [(lo, hi)]:
                nc.vector.tensor_tensor(
                    d3[:, c0 - lo : c1 - lo],
                    win[t][:].indirect(l_n3[:, c0 // 16 : c1 // 16]),
                    hb[t][:, S + c0 : S + c1],
                    ALU.subtract,
                )
            nc.vector.tensor_tensor(d4[:], win[t][:].indirect(l_n4[:, cols]), a_here, ALU.subtract)
            terms[n] = (d3, d4)

        def products(n, t, lo, hi):
            w = hi - lo
            cols = slice(lo // 16, hi // 16)
            d3, d4 = terms[n]
            m3 = tile([P, w], F32, "m3_%d" % n)
            m5 = tile([P, w], F32, "m5_%d" % n)
            nc.vector.scalar_tensor_tensor(m3[:], hb[t][:, lo:hi], 2.0, d3[:], ALU.mult, ALU.mult)
            nc.vector.tensor_tensor(m5[:], hb[t][:].indirect(l_n5[:, cols]), d4[:], ALU.mult)
            terms[n] = (m3, m5)

        def total(n, t, lo, hi):
            m3, m5 = terms[n]
            dst = res[:, S * t + lo : S * t + hi]
            if t < PACK - 1:
                turned_ps = ps.tile([P, S], F32, name="turned_ps%d" % t, tag="bank%d" % t)
                for c in range(0, S, P):
                    for term in (m3, m5):
                        nc.tensor.matmul(
                            turned_ps[:, c : c + P], term[:, c : c + P], ident[:],
                            start=term is m3, stop=term is m5, is_transpose=True,
                        )
                turned = tile([P, S], F32, "turned%d" % t)
                nc.scalar.activation(turned[:], turned_ps[:], ACT.Copy)
                back_ps = ps.tile([P, S], F32, name="back_ps%d" % t, tag="bank%d" % (PACK + t))
                for c in range(0, S, P):
                    nc.tensor.transpose(back_ps[:, c : c + P], turned[:, c : c + P], ident[:])
                nc.scalar.activation(dst, back_ps[:], ACT.Copy)
            else:
                nc.vector.tensor_tensor(dst, m3[:], m5[:], ALU.add)
            nc.sync.dma_start(out_rows[:, t, lo:hi], dst)

        def cast_views(h):
            src = res[:].rearrange("p (t j) -> p t j", t=PACK)[:, :, HALF * h : HALF * (h + 1)]
            return (
                o16[h][:].rearrange("p (c i t) -> p c t i", t=PACK, i=2),
                src.rearrange("p t (c i) -> p c t i", i=2),
            )

        def quantise(h):
            cols = slice(HALF * h, HALF * (h + 1))
            nc.vector.quantize_mx(out=oq_w[:, cols].bitcast(FP8X4), scales=oq_s[:, cols], in_=o16[h][:])
            nc.sync.dma_start(out_w[:, cols], oq_w[:, cols].bitcast(I32))

        for n, step in enumerate(steps):
            if n > 0:
                total(n - 1, *steps[n - 1])
            lookups(n, *step)
            if n == len(steps) - 1:
                dst, src = cast_views(0)
                nc.scalar.activation(dst, src, ACT.Copy)
            products(n, *step)
        dst, src = cast_views(1)
        nc.scalar.activation(dst[:, :, 0:2, :], src[:, :, 0:2, :], ACT.Copy)
        total(len(steps) - 1, *steps[-1])
        quantise(0)
        nc.vector.tensor_copy(dst[:, :, 2:4, :], src[:, :, 2:4, :])
        quantise(1)
        for q in range(4):
            engine = nc.scalar if q % 2 == 0 else nc.sync
            engine.dma_start(out_2[0, 4 * q : 4 * q + 4, :].bitcast(I32), oq_s[32 * q : 32 * q + 4, :].bitcast(I32))
